import numpy as np
import ml_dtypes


def mxq(x, axis, fmt="e4m3"):
    dtype, down = {"e4m3": (ml_dtypes.float8_e4m3fn, 7), "e5m2": (ml_dtypes.float8_e5m2, 14)}[fmt]
    v = np.moveaxis(np.asarray(x, np.float32).astype(ml_dtypes.bfloat16).astype(np.float64), axis, -1)
    blocks = v.reshape(v.shape[:-1] + (-1, 32))
    amax = np.abs(blocks).max(-1, keepdims=True)
    byte = np.maximum(np.where(amax > 0, np.frexp(amax)[1] - 1 + 127, 0) - down, 1)
    scale = np.exp2(byte - 127.0)
    codes = (blocks / scale).astype(np.float32).astype(dtype).astype(np.float64)
    return np.moveaxis((codes * scale).reshape(v.shape), -1, axis)


WIDE = False


def mx_kscale(k):
    if not WIDE:
        return np.ones(k)
    levels = np.array([10, -10, 5, -5, 0])
    if k % 512:
        return np.exp2(np.random.permutation(np.resize(levels, k // 32))).repeat(32)
    a = np.empty((k // 512, 16))
    for p in range(k // 512):
        a[p, :8] = np.random.permutation(np.resize(levels, 8))
        for g in range(8):
            far = levels[np.abs(levels - a[p, g]) >= 10]
            a[p, g + 8] = far[np.random.randint(len(far))]
    return np.exp2(a.ravel()).repeat(32)


def f64(x):
    return np.asarray(x).astype(np.float64)


def striped(idx):
    return np.tile(idx.reshape(-1, 16).T, (8, 1)).astype(np.uint16)


def unstriped(offs):
    return offs[:16].T.reshape(-1).astype(np.int64)


def pack_weight(w):
    k, n = w.shape
    w = f64(np.asarray(w, np.float32).astype(ml_dtypes.bfloat16)).reshape(k // 32, 32, n)
    amax = np.abs(w).max(1)
    byte = np.clip(np.where(amax > 0, np.frexp(amax)[1] - 1 + 127 - 7, 1), 1, 254)
    scaled = (w * np.exp2(127.0 - byte)[:, None, :]).reshape(k, n).astype(np.float32)
    words = np.ascontiguousarray(scaled.reshape(k // 512, 128, 4, n).transpose(0, 1, 3, 2)).astype(ml_dtypes.float8_e4m3fn).view(np.uint8)
    return words, np.ascontiguousarray(byte.astype(np.uint8).reshape(k // 512, 16, n))


def unpack_weight(words, scales):
    g, p, n, _ = words.shape
    vals = np.ascontiguousarray(words).view(ml_dtypes.float8_e4m3fn).astype(np.float64) * np.repeat(np.exp2(scales.astype(np.float64) - 127.0), 8, axis=1)[..., None]
    return vals.transpose(0, 1, 3, 2).reshape(g * 512, n)


K, T, S, D, N, H, V, U = 1024, 2048, 1024, 4, 128, 512, 256, 512


def setup_inputs():
    n = np.random.standard_normal
    s = mx_kscale(K)[:, None]
    u = mx_kscale(H)
    packed_xT = pack_weight(n((K, T)) * s)
    return {
        "x_words": packed_xT[0],
        "x_scales": packed_xT[1],
        "w1": (n((K, H)) / np.sqrt(K) / s).astype(np.float32),
        "w2": (n((K, H)) / np.sqrt(K) / s).astype(np.float32),
        "decay": (np.random.uniform(0.3, 1.0, (H, S))).astype(np.float32),
        "unit": (np.random.uniform(0.6, 1.4, (H, 1)) * u[:, None]).astype(np.float32),
        "w3": (n((H, N)) / np.sqrt(H) / u[:, None]).astype(np.float32),
        "offs": striped(np.random.permutation(T)[:S]),
        "prv": striped(np.random.permutation(S)),
        "tick": striped(np.random.permutation(np.concatenate([np.arange(V), np.random.randint(0, V, U - V)]))),
    }


def reference(x_words, x_scales, w1, w2, decay, unit, w3, offs, prv, tick):
    xq = unpack_weight(x_words, x_scales)[:, unstriped(offs)]
    bd = mxq(f64(w1), 0, "e4m3").T @ xq
    bid = np.log(np.exp(bd) + 1.0)
    bp = bid[:, unstriped(prv)]
    dbid = bid - bp
    ak = mxq(f64(w2), 0, "e4m3").T @ xq
    ask = np.log(np.exp(ak) + 1.0)
    ap = ask[:, unstriped(prv)]
    dask = ask - ap
    wofi = f64(decay) * (dbid - dask)
    ofi = wofi.reshape(len(wofi), -1, D).sum(axis=2)
    ot = ofi[:, unstriped(tick)]
    dp2 = bid + ask
    depth = dp2.reshape(len(dp2), -1, D).sum(axis=2)
    dt = depth[:, unstriped(tick)]
    imp = ot / (dt + 1.0)
    hid = f64(unit) * (3.0 * np.tanh(imp))
    return mxq(f64(w3), 0, "e4m3").T @ mxq(hid, 0, "e4m3")

@@ -1,0 +1,329 @@
+from contextlib import ExitStack
+
+import concourse.mybir as mybir
+from concourse.masks import make_identity
+
+K, T, S, D, N, H, V, U = 1024, 2048, 1024, 4, 128, 512, 256, 512
+FLOPS = 2 * (2 * K * H * S + H * N * U)
+
+F32 = mybir.dt.float32
+BF16 = mybir.dt.bfloat16
+I32 = mybir.dt.int32
+U32 = mybir.dt.uint32
+U16 = mybir.dt.uint16
+U8 = mybir.dt.uint8
+FP8X4 = mybir.dt.float8_e4m3fn_x4
+ALU = mybir.AluOpType
+ACT = mybir.ActivationFunctionType
+
+P = 128
+PACK = 4
+PASSES = K // (P * PACK)
+HALF = 512
+HALVES = S // HALF
+LN_FLOOR = 2.0 ** -60
+
+
+def tile_picked_yofimb_tanh_p_kernel(
+    tc, x_words, x_scales, w1, w2, decay, unit, w3, offs, prv, tick, out
+):
+    nc = tc.nc
+    with ExitStack() as ctx:
+        keep = ctx.enter_context(tc.tile_pool(name="keep", bufs=1))
+        psum = ctx.enter_context(tc.psum_pool(name="psum", bufs=1))
+
+        offs_sb = keep.tile([P, S // 16], U16, name="offs_sb")
+        prv_sb = keep.tile([P, S // 16], U16, name="prv_sb")
+        tick_sb = keep.tile([P, U // 16], U16, name="tick_sb")
+        x_table = [keep.tile([P, T], U32, name="x_table%d" % o) for o in range(PASSES)]
+        scale_table = keep.tile([P, T], U8, name="scale_table")
+        weights = (w1, w2)
+        w_raw = [[keep.tile([P, PACK, H], F32, name="w_raw%d%d" % (m, o)) for o in range(PASSES)] for m in range(2)]
+        decay_sb = [keep.tile([P, S], F32, name="decay%d" % t) for t in range(PACK)]
+        unit_sb = keep.tile([P, PACK], F32, name="unit_sb")
+        w3_raw = keep.tile([P, PACK, N], F32, name="w3_raw")
+
+        def load_words(o):
+            nc.sync.dma_start(x_table[o][:].bitcast(I32), x_words[o].rearrange("p c r -> p (c r)").bitcast(I32))
+
+        def load_weight(m, o):
+            rows = weights[m][o * P * PACK : (o + 1) * P * PACK, :]
+            nc.sync.dma_start(w_raw[m][o][:], rows.rearrange("(p j) c -> p j c", j=PACK))
+
+        nc.vector.memset(scale_table[:].bitcast(I32), 0)
+        nc.sync.dma_start(offs_sb[:], offs)
+        load_weight(0, 0)
+        load_words(0)
+        for q in range(4):
+            nc.sync.dma_start(
+                scale_table[32 * q : 32 * q + 4 * PASSES, :].bitcast(I32),
+                x_scales[:, 4 * q : 4 * q + 4, :].bitcast(I32),
+            )
+        load_words(1)
+        load_weight(0, 1)
+        load_weight(1, 0)
+        load_weight(1, 1)
+        nc.sync.dma_start(prv_sb[:], prv)
+        nc.sync.dma_start(tick_sb[:], tick)
+        nc.sync.dma_start(unit_sb[:], unit.rearrange("(p t) o -> p (t o)", t=PACK))
+        nc.sync.dma_start(w3_raw[:], w3.rearrange("(p j) n -> p j n", j=PACK))
+        decay_dealt = decay.rearrange("(p t) j -> t p j", t=PACK)
+        for t in range(PACK):
+            nc.sync.dma_start(decay_sb[t][:], decay_dealt[t])
+
+        x_codes = {}
+        x_bytes = {}
+
+        def gather_words(o, h):
+            x_codes[o, h] = keep.tile([P, HALF], U32, name="x_codes%d%d" % (o, h), align_bytes=64)
+            nc.vector.tensor_copy(x_codes[o, h][:], x_table[o][:].indirect(offs_sb[:, h * 32 : (h + 1) * 32]))
+
+        def gather_bytes(h):
+            x_bytes[h] = keep.tile([P, HALF], U8, name="x_bytes%d" % h, align_bytes=64)
+            nc.vector.tensor_copy(x_bytes[h][:], scale_table[:].indirect(offs_sb[:, h * 32 : (h + 1) * 32]))
+
+        w_round = {}
+        w_codes = {}
+        w_bytes = {}
+
+        def round_weight(m, o, g, on_vector):
+            w_round[m, o, g] = keep.tile([P, 2 * P * PACK], BF16, name="w_round%d%d%d" % (m, o, g), align_bytes=64)
+            dst = w_round[m, o, g][:].rearrange("p (t c j) -> p c t j", t=2, j=PACK)
+            src = w_raw[m][o][:].rearrange("p j (c t) -> p c t j", t=PACK)[:, :, 2 * g : 2 * g + 2, :]
+            if on_vector:
+                nc.vector.tensor_copy(dst, src)
+            else:
+                nc.scalar.copy(dst, src)
+
+        def quantise_weight(m, o, g):
+            w_codes[m, o, g] = keep.tile([P, 2 * P], U32, name="w_codes%d%d%d" % (m, o, g), align_bytes=64)
+            w_bytes[m, o, g] = keep.tile([P, 2 * P], U8, name="w_bytes%d%d%d" % (m, o, g), align_bytes=64)
+            nc.vector.quantize_mx(
+                out=w_codes[m, o, g][:].bitcast(FP8X4), scales=w_bytes[m, o, g][:], in_=w_round[m, o, g][:]
+            )
+
+        round_weight(0, 0, 0, False)
+        gather_words(0, 0)
+        gather_words(0, 1)
+        round_weight(0, 0, 1, False)
+        quantise_weight(0, 0, 0)
+        gather_bytes(0)
+        gather_bytes(1)
+        gather_words(1, 0)
+        gather_words(1, 1)
+        round_weight(0, 1, 0, False)
+        quantise_weight(0, 1, 0)
+        round_weight(1, 0, 0, False)
+        quantise_weight(1, 0, 0)
+        round_weight(1, 1, 0, True)
+        quantise_weight(1, 1, 0)
+
+        banks = {}
+
+        def product(m, t, h, o):
+            g, tl = divmod(t, 2)
+            if o == 0:
+                banks[m, t, h] = psum.tile([P, HALF], F32, name="bank", tag="bank%d%d%d" % (m, tl, h))
+            cols = slice(tl * P, (tl + 1) * P)
+            nc.tensor.matmul_mx(
+                out=banks[m, t, h][:],
+                lhsT=w_codes[m, o, g][:, cols].bitcast(FP8X4),
+                lhsT_scale=w_bytes[m, o, g][:, cols],
+                rhs=x_codes[o, h][:].bitcast(FP8X4),
+                rhs_scale=x_bytes[h][4 * o : P, :],
+                start=(o == 0),
+                stop=(o == PASSES - 1),
+            )
+
+        sig = keep.tile([P, 8 * HALF], F32, name="sig")
+        soft = [keep.tile([P, 4, HALF], F32, name="soft%d" % t) for t in range(PACK)]
+        diff = [keep.tile([P, S], F32, name="diff%d" % t) for t in range(PACK)]
+        flow = [keep.tile([P, S], F32, name="flow%d" % t) for t in range(PACK)]
+        book = [keep.tile([P, 2 * V], F32, name="book%d" % t) for t in range(PACK)]
+        inverse = keep.tile([P, PACK, V], F32, name="inverse")
+        gain = keep.tile([P, PACK], F32, name="gain")
+        ident = keep.tile([P, P], F32, name="ident")
+        make_identity(nc, ident[:])
+        striped = sig[:].rearrange("p (c k x) -> p c k x", c=2, k=8)
+
+        def sigmoid(m, t, h):
+            k = (t % 2) * 4 + m * 2 + h
+            src = banks[m, t, h][:].rearrange("p (v c e) -> p c e v", c=2, e=2)
+            if t < 2:
+                dst = sig[:, k * HALF : (k + 1) * HALF].rearrange("p (c e v) -> p c e v", c=2, e=2)
+            else:
+                dst = striped[:, :, k, :].rearrange("p c (e v) -> p c e v", e=2)
+            nc.scalar.activation(dst, src, ACT.Sigmoid, scale=-1.0)
+
+        def logarithm(t):
+            dst = soft[t][:].rearrange("p k (c x) -> p c k x", c=2)
+            if t < 2:
+                src = sig[:, t * 4 * HALF : (t + 1) * 4 * HALF].rearrange("p (k c x) -> p c k x", k=4, c=2)
+            else:
+                src = striped[:, :, (t % 2) * 4 : (t % 2) * 4 + 4, :]
+            nc.scalar.activation(dst, src, ACT.Ln, bias=LN_FLOOR)
+
+        def softplus(m, t, h):
+            part = soft[t][:, m * 2 + h, :].rearrange("p (d v) -> p d v", d=D)
+            raw = banks[m, t, h][:].rearrange("p (v d) -> p d v", d=D)
+            nc.vector.scalar_tensor_tensor(part, part, -1.0, raw, ALU.mult, ALU.max)
+
+        def differ(t):
+            for h in range(HALVES):
+                sides = [soft[t][:, m * 2 + h, :].rearrange("p (d c i) -> p c d i", d=D, i=4) for m in range(2)]
+                dst = diff[t][:, h * HALF : (h + 1) * HALF].rearrange("p (c i d) -> p c d i", d=D, i=4)
+                nc.vector.tensor_tensor(dst, sides[0], sides[1], ALU.subtract)
+
+        def fetch_earlier(t, h, on_vector):
+            src = diff[t][:].indirect(prv_sb[:, h * 32 : (h + 1) * 32])
+            dst = flow[t][:, h * HALF : (h + 1) * HALF]
+            if on_vector:
+                nc.vector.tensor_copy(dst, src)
+            else:
+                nc.scalar.activation(dst, src, ACT.Copy)
+
+        def weigh(t):
+            nc.vector.tensor_tensor(flow[t][:], diff[t][:], flow[t][:], ALU.subtract)
+            nc.vector.tensor_tensor(
+                diff[t][:].rearrange("p (h d v) -> p h v d", h=HALVES, d=D),
+                flow[t][:].rearrange("p (h v d) -> p h v d", h=HALVES, d=D),
+                decay_sb[t][:].rearrange("p (h v d) -> p h v d", h=HALVES, d=D),
+                ALU.mult,
+            )
+
+        def add_turned(dst, blocks):
+            for n, block in enumerate(blocks):
+                nc.tensor.matmul(dst, block, ident[:], start=(n == 0), stop=(n == len(blocks) - 1), is_transpose=True)
+
+        def sum_depth(bank, t):
+            for h in range(HALVES):
+                blocks = [soft[t][:, m * 2 + h, d * P : (d + 1) * P] for m in range(2) for d in range(D)]
+                add_turned(bank[:, (t % 2) * 2 + h, :], blocks)
+
+        def sum_flow(bank, t):
+            for h in range(HALVES):
+                blocks = [diff[t][:, (h * D + d) * P : (h * D + d + 1) * P] for d in range(D)]
+                add_turned(bank[:, (t % 2) * 2 + h, :], blocks)
+
+        first = [(0, 0), (0, 1), (1, 0), (1, 1)]
+        for o in range(PASSES):
+            for t, h in first:
+                product(0, t, h, o)
+        for t, h in first:
+            sigmoid(0, t, h)
+        ask_order = [(1, 0), (0, 0), (1, 1), (0, 1)]
+        for o in range(PASSES):
+            for t, h in ask_order:
+                product(1, t, h, o)
+        for t, h in ask_order:
+            sigmoid(1, t, h)
+
+        round_weight(0, 1, 1, True)
+        quantise_weight(0, 0, 1)
+        round_weight(1, 0, 1, True)
+        quantise_weight(0, 1, 1)
+        round_weight(1, 1, 1, True)
+        quantise_weight(1, 0, 1)
+        w3_round = keep.tile([P, N * PACK], BF16, name="w3_round", align_bytes=64)
+        w3_codes = keep.tile([P, N], U32, name="w3_codes", align_bytes=64)
+        w3_bytes = keep.tile([P, N], U8, name="w3_bytes", align_bytes=64)
+        nc.vector.tensor_copy(
+            w3_round[:].rearrange("p (n j) -> p n j", j=PACK), w3_raw[:].rearrange("p j n -> p n j")
+        )
+        quantise_weight(1, 1, 1)
+        nc.vector.tensor_scalar(gain[:], unit_sb[:], 3.0, None, ALU.mult)
+        nc.vector.quantize_mx(out=w3_codes[:].bitcast(FP8X4), scales=w3_bytes[:], in_=w3_round[:])
+
+        units = [(m, h) for h in range(HALVES) for m in range(2)]
+        for t in range(2):
+            logarithm(t)
+        for t in range(2):
+            for m, h in units:
+                softplus(m, t, h)
+                for o in range(PASSES):
+                    product(m, t + 2, h, o)
+        for m, h in units[:3]:
+            sigmoid(m, 2, h)
+        for m, h in units:
+            sigmoid(m, 3, h)
+        sigmoid(units[3][0], 2, units[3][1])
+        differ(0)
+        differ(1)
+        fetch_earlier(0, 0, True)
+        fetch_earlier(0, 1, True)
+        fetch_earlier(1, 0, False)
+        fetch_earlier(1, 1, False)
+        weigh(0)
+        weigh(1)
+
+        for t in (2, 3):
+            logarithm(t)
+        for t in (2, 3):
+            for m, h in units:
+                softplus(m, t, h)
+            differ(t)
+            fetch_earlier(t, 0, False)
+            fetch_earlier(t, 1, False)
+
+        depth_banks = [psum.tile([P, 4, P], F32, name="depth_bank", tag="bank%d00" % g) for g in range(2)]
+        flow_banks = [psum.tile([P, 4, P], F32, name="flow_bank", tag=tag) for tag in ("bank001", "bank101", "bank010")]
+        flow_bank_of = [flow_banks[0], flow_banks[0], flow_banks[1], flow_banks[2]]
+        for t in range(PACK):
+            sum_depth(depth_banks[t // 2], t)
+        for g in range(2):
+            nc.scalar.activation(
+                inverse[:, 2 * g : 2 * g + 2, :].rearrange("p t v -> p (t v)"),
+                depth_banks[g][:].rearrange("p k i -> p (k i)"),
+                ACT.Ln,
+                bias=1.0,
+            )
+        nc.scalar.activation(inverse[:], inverse[:], ACT.Exp, scale=-1.0)
+        sum_flow(flow_bank_of[0], 0)
+        sum_flow(flow_bank_of[1], 1)
+        for t in (2, 3):
+            weigh(t)
+            sum_flow(flow_bank_of[t], t)
+
+        picked = keep.tile([P, PACK, U], F32, name="picked")
+        back_tags = ["bank110", "bank011", "bank111", "bank110"]
+        for t in range(PACK):
+            ratio = book[t][:, V : 2 * V]
+            k = (t % 2) * 2
+            nc.vector.tensor_tensor(
+                ratio, flow_bank_of[t][:, k : k + 2, :].rearrange("p k i -> p (k i)"), inverse[:, t, :], ALU.mult
+            )
+            nc.scalar.activation(ratio, ratio, ACT.Tanh)
+            back = psum.tile([P, V], F32, name="back", tag=back_tags[t])
+            for h in range(HALVES):
+                nc.tensor.transpose(back[:, h * P : (h + 1) * P], ratio[:, h * P : (h + 1) * P], ident[:])
+            nc.scalar.activation(book[t][:, 0:V], back[:], ACT.Copy, scale=gain[:, t : t + 1])
+            for r in range(2):
+                src = book[t][:].indirect(tick_sb[:, r * 16 : (r + 1) * 16])
+                dst = picked[:, t, r * 256 : (r + 1) * 256]
+                if t == PACK - 1 and r == 0:
+                    nc.vector.tensor_copy(dst, src)
+                else:
+                    nc.scalar.activation(dst, src, ACT.Copy)
+
+        for r in range(2):
+            cols = slice(r * 256, (r + 1) * 256)
+            hid_round = keep.tile([P, 256 * PACK], BF16, name="hid_round%d" % r, align_bytes=64)
+            hid_codes = keep.tile([P, 256], U32, name="hid_codes%d" % r, align_bytes=64)
+            hid_bytes = keep.tile([P, 256], U8, name="hid_bytes%d" % r, align_bytes=64)
+            nc.vector.tensor_copy(
+                hid_round[:].rearrange("p (r t) -> p r t", t=PACK), picked[:, :, cols].rearrange("p t r -> p r t")
+            )
+            nc.vector.quantize_mx(out=hid_codes[:].bitcast(FP8X4), scales=hid_bytes[:], in_=hid_round[:])
+            last = psum.tile([P, 256], F32, name="last", tag="bank%d00" % r)
+            nc.tensor.matmul_mx(
+                out=last[:],
+                lhsT=w3_codes[:].bitcast(FP8X4),
+                lhsT_scale=w3_bytes[:],
+                rhs=hid_codes[:].bitcast(FP8X4),
+                rhs_scale=hid_bytes[:],
+                start=True,
+                stop=True,
+            )
+            result = keep.tile([P, 256], F32, name="result%d" % r)
+            nc.scalar.copy(result[:], last[:])
+            nc.sync.dma_start(out[:, cols], result[:])

@@ -51,8 +51,10 @@ def tile_picked_yofimb_tanh_p_kernel(
             nc.sync.dma_start(w_raw[m][o][:], rows.rearrange("(p j) c -> p j c", j=PACK))
 
         nc.vector.memset(scale_table[:].bitcast(I32), 0)
+        warm = keep.tile([P, 2], F32, name="warm")
+        nc.vector.memset(warm[:, 0:1], 0.0)
+        nc.scalar.activation(warm[:, 1:2], warm[:, 0:1], ACT.Sigmoid, scale=-1.0)
         nc.sync.dma_start(offs_sb[:], offs)
-        load_weight(0, 0)
         load_words(0)
         for q in range(4):
             nc.sync.dma_start(
@@ -60,6 +62,7 @@ def tile_picked_yofimb_tanh_p_kernel(
                 x_scales[:, 4 * q : 4 * q + 4, :].bitcast(I32),
             )
         load_words(1)
+        load_weight(0, 0)
         load_weight(0, 1)
         load_weight(1, 0)
         load_weight(1, 1)
@@ -102,21 +105,21 @@ def tile_picked_yofimb_tanh_p_kernel(
                 out=w_codes[m, o, g][:].bitcast(FP8X4), scales=w_bytes[m, o, g][:], in_=w_round[m, o, g][:]
             )
 
-        round_weight(0, 0, 0, False)
         gather_words(0, 0)
         gather_words(0, 1)
-        round_weight(0, 0, 1, False)
-        quantise_weight(0, 0, 0)
         gather_bytes(0)
-        gather_bytes(1)
         gather_words(1, 0)
+        gather_bytes(1)
         gather_words(1, 1)
+        round_weight(0, 0, 0, False)
+        quantise_weight(0, 0, 0)
         round_weight(0, 1, 0, False)
         quantise_weight(0, 1, 0)
         round_weight(1, 0, 0, False)
         quantise_weight(1, 0, 0)
         round_weight(1, 1, 0, True)
         quantise_weight(1, 1, 0)
+        round_weight(0, 0, 1, False)
 
         banks = {}
 
@@ -144,33 +147,26 @@ def tile_picked_yofimb_tanh_p_kernel(
         gain = keep.tile([P, PACK], F32, name="gain")
         ident = keep.tile([P, P], F32, name="ident")
         make_identity(nc, ident[:])
-        striped = sig[:].rearrange("p (c k x) -> p c k x", c=2, k=8)
 
         def sigmoid(m, t, h):
-            k = (t % 2) * 4 + m * 2 + h
-            src = banks[m, t, h][:].rearrange("p (v c e) -> p c e v", c=2, e=2)
-            if t < 2:
-                dst = sig[:, k * HALF : (k + 1) * HALF].rearrange("p (c e v) -> p c e v", c=2, e=2)
-            else:
-                dst = striped[:, :, k, :].rearrange("p c (e v) -> p c e v", e=2)
+            k = (t % 2) * 4 + h * 2 + m
+            src = banks[m, t, h][:].rearrange("p (v d) -> p d v", d=D)
+            dst = sig[:, k * HALF : (k + 1) * HALF].rearrange("p (d v) -> p d v", d=D)
             nc.scalar.activation(dst, src, ACT.Sigmoid, scale=-1.0)
 
-        def logarithm(t):
-            dst = soft[t][:].rearrange("p k (c x) -> p c k x", c=2)
-            if t < 2:
-                src = sig[:, t * 4 * HALF : (t + 1) * 4 * HALF].rearrange("p (k c x) -> p c k x", k=4, c=2)
-            else:
-                src = striped[:, :, (t % 2) * 4 : (t % 2) * 4 + 4, :]
-            nc.scalar.activation(dst, src, ACT.Ln, bias=LN_FLOOR)
+        def logarithm(t, h):
+            k = (t % 2) * 4 + h * 2
+            dst = soft[t][:, h * 2 : h * 2 + 2, :].rearrange("p m c -> p (m c)")
+            nc.scalar.activation(dst, sig[:, k * HALF : (k + 2) * HALF], ACT.Ln, bias=LN_FLOOR)
 
         def softplus(m, t, h):
-            part = soft[t][:, m * 2 + h, :].rearrange("p (d v) -> p d v", d=D)
+            part = soft[t][:, h * 2 + m, :].rearrange("p (d v) -> p d v", d=D)
             raw = banks[m, t, h][:].rearrange("p (v d) -> p d v", d=D)
             nc.vector.scalar_tensor_tensor(part, part, -1.0, raw, ALU.mult, ALU.max)
 
         def differ(t):
             for h in range(HALVES):
-                sides = [soft[t][:, m * 2 + h, :].rearrange("p (d c i) -> p c d i", d=D, i=4) for m in range(2)]
+                sides = [soft[t][:, h * 2 + m, :].rearrange("p (d c i) -> p c d i", d=D, i=4) for m in range(2)]
                 dst = diff[t][:, h * HALF : (h + 1) * HALF].rearrange("p (c i d) -> p c d i", d=D, i=4)
                 nc.vector.tensor_tensor(dst, sides[0], sides[1], ALU.subtract)
 
@@ -197,7 +193,7 @@ def tile_picked_yofimb_tanh_p_kernel(
 
         def sum_depth(bank, t):
             for h in range(HALVES):
-                blocks = [soft[t][:, m * 2 + h, d * P : (d + 1) * P] for m in range(2) for d in range(D)]
+                blocks = [soft[t][:, h * 2 + m, d * P : (d + 1) * P] for m in range(2) for d in range(D)]
                 add_turned(bank[:, (t % 2) * 2 + h, :], blocks)
 
         def sum_flow(bank, t):
@@ -211,7 +207,7 @@ def tile_picked_yofimb_tanh_p_kernel(
                 product(0, t, h, o)
         for t, h in first:
             sigmoid(0, t, h)
-        ask_order = [(1, 0), (0, 0), (1, 1), (0, 1)]
+        ask_order = first[::-1]
         for o in range(PASSES):
             for t, h in ask_order:
                 product(1, t, h, o)
@@ -235,8 +231,8 @@ def tile_picked_yofimb_tanh_p_kernel(
         nc.vector.quantize_mx(out=w3_codes[:].bitcast(FP8X4), scales=w3_bytes[:], in_=w3_round[:])
 
         units = [(m, h) for h in range(HALVES) for m in range(2)]
-        for t in range(2):
-            logarithm(t)
+        for t, h in first:
+            logarithm(t, h)
         for t in range(2):
             for m, h in units:
                 softplus(m, t, h)
@@ -256,17 +252,17 @@ def tile_picked_yofimb_tanh_p_kernel(
         weigh(0)
         weigh(1)
 
+        for t, h in ((2, 1), (2, 0), (3, 0), (3, 1)):
+            logarithm(t, h)
         for t in (2, 3):
-            logarithm(t)
-        for t in (2, 3):
-            for m, h in units:
+            for m, h in units[::-1] if t == 2 else units:
                 softplus(m, t, h)
             differ(t)
-            fetch_earlier(t, 0, False)
+            fetch_earlier(t, 0, t == 3)
             fetch_earlier(t, 1, False)
 
-        depth_banks = [psum.tile([P, 4, P], F32, name="depth_bank", tag="bank%d00" % g) for g in range(2)]
-        flow_banks = [psum.tile([P, 4, P], F32, name="flow_bank", tag=tag) for tag in ("bank001", "bank101", "bank010")]
+        depth_banks = [psum.tile([P, 4, P], F32, name="depth_bank", tag="bank%d01" % (1 - g)) for g in range(2)]
+        flow_banks = [psum.tile([P, 4, P], F32, name="flow_bank", tag=tag) for tag in ("bank100", "bank000", "bank010")]
         flow_bank_of = [flow_banks[0], flow_banks[0], flow_banks[1], flow_banks[2]]
         for t in range(PACK):
             sum_depth(depth_banks[t // 2], t)
@@ -280,13 +276,10 @@ def tile_picked_yofimb_tanh_p_kernel(
         nc.scalar.activation(inverse[:], inverse[:], ACT.Exp, scale=-1.0)
         sum_flow(flow_bank_of[0], 0)
         sum_flow(flow_bank_of[1], 1)
-        for t in (2, 3):
-            weigh(t)
-            sum_flow(flow_bank_of[t], t)
 
         picked = keep.tile([P, PACK, U], F32, name="picked")
         back_tags = ["bank110", "bank011", "bank111", "bank110"]
-        for t in range(PACK):
+        def finish(t):
             ratio = book[t][:, V : 2 * V]
             k = (t % 2) * 2
             nc.vector.tensor_tensor(
@@ -297,13 +290,28 @@ def tile_picked_yofimb_tanh_p_kernel(
             for h in range(HALVES):
                 nc.tensor.transpose(back[:, h * P : (h + 1) * P], ratio[:, h * P : (h + 1) * P], ident[:])
             nc.scalar.activation(book[t][:, 0:V], back[:], ACT.Copy, scale=gain[:, t : t + 1])
-            for r in range(2):
-                src = book[t][:].indirect(tick_sb[:, r * 16 : (r + 1) * 16])
-                dst = picked[:, t, r * 256 : (r + 1) * 256]
-                if t == PACK - 1 and r == 0:
-                    nc.vector.tensor_copy(dst, src)
-                else:
-                    nc.scalar.activation(dst, src, ACT.Copy)
+
+        def fetch_ticks(t, r, on_vector):
+            src = book[t][:].indirect(tick_sb[:, r * 16 : (r + 1) * 16])
+            dst = picked[:, t, r * 256 : (r + 1) * 256]
+            if on_vector:
+                nc.vector.tensor_copy(dst, src)
+            else:
+                nc.scalar.activation(dst, src, ACT.Copy)
+
+        for t in range(2):
+            finish(t)
+            fetch_ticks(t, 0, False)
+            fetch_ticks(t, 1, False)
+        for t in (2, 3):
+            weigh(t)
+            sum_flow(flow_bank_of[t], t)
+        finish(2)
+        finish(3)
+        for r in range(2):
+            fetch_ticks(2, r, True)
+        fetch_ticks(3, 0, False)
+        fetch_ticks(3, 1, False)
 
         for r in range(2):
             cols = slice(r * 256, (r + 1) * 256)
@@ -314,7 +322,7 @@ def tile_picked_yofimb_tanh_p_kernel(
                 hid_round[:].rearrange("p (r t) -> p r t", t=PACK), picked[:, :, cols].rearrange("p t r -> p r t")
             )
             nc.vector.quantize_mx(out=hid_codes[:].bitcast(FP8X4), scales=hid_bytes[:], in_=hid_round[:])
-            last = psum.tile([P, 256], F32, name="last", tag="bank%d00" % r)
+            last = psum.tile([P, 256], F32, name="last", tag="bank%d01" % r)
             nc.tensor.matmul_mx(
                 out=last[:],
                 lhsT=w3_codes[:].bitcast(FP8X4),

@@ -123,10 +123,10 @@ def tile_picked_yofimb_tanh_p_kernel(
 
         banks = {}
 
-        def product(m, t, h, o):
+        def product(m, t, h, o, bank):
             g, tl = divmod(t, 2)
             if o == 0:
-                banks[m, t, h] = psum.tile([P, HALF], F32, name="bank", tag="bank%d%d%d" % (m, tl, h))
+                banks[m, t, h] = psum.tile([P, HALF], F32, name="bank", tag="bank%d" % bank)
             cols = slice(tl * P, (tl + 1) * P)
             nc.tensor.matmul_mx(
                 out=banks[m, t, h][:],
@@ -144,9 +144,10 @@ def tile_picked_yofimb_tanh_p_kernel(
         flow = [keep.tile([P, S], F32, name="flow%d" % t) for t in range(PACK)]
         book = [keep.tile([P, 2 * V], F32, name="book%d" % t) for t in range(PACK)]
         inverse = keep.tile([P, PACK, V], F32, name="inverse")
-        gain = keep.tile([P, PACK], F32, name="gain")
         ident = keep.tile([P, P], F32, name="ident")
         make_identity(nc, ident[:])
+        parked = keep.tile([P, D, P], F32, name="parked")
+        parked_unit = (0, 2, 0)
 
         def sigmoid(m, t, h):
             k = (t % 2) * 4 + h * 2 + m
@@ -161,14 +162,20 @@ def tile_picked_yofimb_tanh_p_kernel(
 
         def softplus(m, t, h):
             part = soft[t][:, h * 2 + m, :].rearrange("p (d v) -> p d v", d=D)
-            raw = banks[m, t, h][:].rearrange("p (v d) -> p d v", d=D)
+            if (m, t, h) == parked_unit:
+                raw = parked[:]
+            else:
+                raw = banks[m, t, h][:].rearrange("p (v d) -> p d v", d=D)
             nc.vector.scalar_tensor_tensor(part, part, -1.0, raw, ALU.mult, ALU.max)
 
         def differ(t):
-            for h in range(HALVES):
-                sides = [soft[t][:, h * 2 + m, :].rearrange("p (d c i) -> p c d i", d=D, i=4) for m in range(2)]
-                dst = diff[t][:, h * HALF : (h + 1) * HALF].rearrange("p (c i d) -> p c d i", d=D, i=4)
-                nc.vector.tensor_tensor(dst, sides[0], sides[1], ALU.subtract)
+            dealt = flow[t][:].rearrange("p (h c) -> p h c", h=HALVES)
+            sides = soft[t][:].rearrange("p (h m) c -> p m h c", m=2)
+            nc.vector.tensor_tensor(dealt, sides[:, 0], sides[:, 1], ALU.subtract)
+            nc.vector.tensor_copy(
+                diff[t][:].rearrange("p (h v d) -> p h v d", h=HALVES, d=D),
+                flow[t][:].rearrange("p (h d v) -> p h v d", h=HALVES, d=D),
+            )
 
         def fetch_earlier(t, h, on_vector):
             src = diff[t][:].indirect(prv_sb[:, h * 32 : (h + 1) * 32])
@@ -178,14 +185,9 @@ def tile_picked_yofimb_tanh_p_kernel(
             else:
                 nc.scalar.activation(dst, src, ACT.Copy)
 
-        def weigh(t):
-            nc.vector.tensor_tensor(flow[t][:], diff[t][:], flow[t][:], ALU.subtract)
-            nc.vector.tensor_tensor(
-                diff[t][:].rearrange("p (h d v) -> p h v d", h=HALVES, d=D),
-                flow[t][:].rearrange("p (h v d) -> p h v d", h=HALVES, d=D),
-                decay_sb[t][:].rearrange("p (h v d) -> p h v d", h=HALVES, d=D),
-                ALU.mult,
-            )
+        def weigh(t, cols):
+            nc.vector.tensor_tensor(flow[t][:, cols], diff[t][:, cols], flow[t][:, cols], ALU.subtract)
+            nc.vector.tensor_tensor(flow[t][:, cols], flow[t][:, cols], decay_sb[t][:, cols], ALU.mult)
 
         def add_turned(dst, blocks):
             for n, block in enumerate(blocks):
@@ -198,19 +200,19 @@ def tile_picked_yofimb_tanh_p_kernel(
 
         def sum_flow(bank, t):
             for h in range(HALVES):
-                blocks = [diff[t][:, (h * D + d) * P : (h * D + d + 1) * P] for d in range(D)]
+                blocks = [flow[t][:, h * HALF + d : (h + 1) * HALF : D] for d in range(D)]
                 add_turned(bank[:, (t % 2) * 2 + h, :], blocks)
 
         first = [(0, 0), (0, 1), (1, 0), (1, 1)]
         for o in range(PASSES):
             for t, h in first:
-                product(0, t, h, o)
+                product(0, t, h, o, t * 4 + h * 2)
         for t, h in first:
             sigmoid(0, t, h)
         ask_order = first[::-1]
         for o in range(PASSES):
             for t, h in ask_order:
-                product(1, t, h, o)
+                product(1, t, h, o, t * 4 + h * 2 + 1)
         for t, h in ask_order:
             sigmoid(1, t, h)
 
@@ -227,69 +229,78 @@ def tile_picked_yofimb_tanh_p_kernel(
             w3_round[:].rearrange("p (n j) -> p n j", j=PACK), w3_raw[:].rearrange("p j n -> p n j")
         )
         quantise_weight(1, 1, 1)
-        nc.vector.tensor_scalar(gain[:], unit_sb[:], 3.0, None, ALU.mult)
         nc.vector.quantize_mx(out=w3_codes[:].bitcast(FP8X4), scales=w3_bytes[:], in_=w3_round[:])
 
         units = [(m, h) for h in range(HALVES) for m in range(2)]
         for t, h in first:
             logarithm(t, h)
-        for t in range(2):
-            for m, h in units:
-                softplus(m, t, h)
+        second = [(m, 2, h) for m, h in units[:3]] + [(m, 3, h) for m, h in units] + [(units[3][0], 2, units[3][1])]
+        for n, (t, (m, h)) in enumerate((t, unit_mh) for t in range(2) for unit_mh in units):
+            softplus(m, t, h)
+            if n > 0:
                 for o in range(PASSES):
-                    product(m, t + 2, h, o)
-        for m, h in units[:3]:
-            sigmoid(m, 2, h)
-        for m, h in units:
-            sigmoid(m, 3, h)
-        sigmoid(units[3][0], 2, units[3][1])
+                    product(*second[n - 1], o, n)
+        sigmoid(*second[0])
+        nc.vector.tensor_copy(parked[:], banks[parked_unit][:].rearrange("p (v d) -> p d v", d=D))
+        for o in range(PASSES):
+            product(*second[7], o, 1)
+        for unit_mth in second[1:]:
+            sigmoid(*unit_mth)
+
+        def log_depth(g, bank):
+            nc.scalar.activation(
+                inverse[:, 2 * g : 2 * g + 2, :].rearrange("p t v -> p (t v)"),
+                bank[:].rearrange("p k i -> p (k i)"),
+                ACT.Ln,
+                bias=1.0,
+            )
+
+        depth_first = psum.tile([P, 4, P], F32, name="depth_first", tag="bank0")
+        sum_depth(depth_first, 0)
+        sum_depth(depth_first, 1)
+        whole = slice(0, S)
         differ(0)
         differ(1)
         fetch_earlier(0, 0, True)
         fetch_earlier(0, 1, True)
         fetch_earlier(1, 0, False)
         fetch_earlier(1, 1, False)
-        weigh(0)
-        weigh(1)
+        weigh(0, whole)
+        weigh(1, whole)
 
-        for t, h in ((2, 1), (2, 0), (3, 0), (3, 1)):
-            logarithm(t, h)
+        logarithm(2, 1)
+        logarithm(2, 0)
+        log_depth(0, depth_first)
+        logarithm(3, 0)
+        logarithm(3, 1)
+        depth_second = psum.tile([P, 4, P], F32, name="depth_second", tag="bank1")
         for t in (2, 3):
             for m, h in units[::-1] if t == 2 else units:
                 softplus(m, t, h)
+            sum_depth(depth_second, t)
             differ(t)
-            fetch_earlier(t, 0, t == 3)
+            fetch_earlier(t, 0, False)
             fetch_earlier(t, 1, False)
-
-        depth_banks = [psum.tile([P, 4, P], F32, name="depth_bank", tag="bank%d01" % (1 - g)) for g in range(2)]
-        flow_banks = [psum.tile([P, 4, P], F32, name="flow_bank", tag=tag) for tag in ("bank100", "bank000", "bank010")]
-        flow_bank_of = [flow_banks[0], flow_banks[0], flow_banks[1], flow_banks[2]]
-        for t in range(PACK):
-            sum_depth(depth_banks[t // 2], t)
-        for g in range(2):
-            nc.scalar.activation(
-                inverse[:, 2 * g : 2 * g + 2, :].rearrange("p t v -> p (t v)"),
-                depth_banks[g][:].rearrange("p k i -> p (k i)"),
-                ACT.Ln,
-                bias=1.0,
-            )
+        log_depth(1, depth_second)
         nc.scalar.activation(inverse[:], inverse[:], ACT.Exp, scale=-1.0)
+        flow_banks = [psum.tile([P, 4, P], F32, name="flow_bank", tag=tag) for tag in ("bank0", "bank2", "bank3")]
+        flow_bank_of = [flow_banks[0], flow_banks[0], flow_banks[1], flow_banks[2]]
         sum_flow(flow_bank_of[0], 0)
         sum_flow(flow_bank_of[1], 1)
 
         picked = keep.tile([P, PACK, U], F32, name="picked")
-        back_tags = ["bank110", "bank011", "bank111", "bank110"]
+        back_tags = ["bank4", "bank5", "bank6", "bank7"]
         def finish(t):
             ratio = book[t][:, V : 2 * V]
             k = (t % 2) * 2
             nc.vector.tensor_tensor(
                 ratio, flow_bank_of[t][:, k : k + 2, :].rearrange("p k i -> p (k i)"), inverse[:, t, :], ALU.mult
             )
-            nc.scalar.activation(ratio, ratio, ACT.Tanh)
             back = psum.tile([P, V], F32, name="back", tag=back_tags[t])
             for h in range(HALVES):
                 nc.tensor.transpose(back[:, h * P : (h + 1) * P], ratio[:, h * P : (h + 1) * P], ident[:])
-            nc.scalar.activation(book[t][:, 0:V], back[:], ACT.Copy, scale=gain[:, t : t + 1])
+            nc.scalar.activation(book[t][:, 0:V], back[:], ACT.Tanh)
+            nc.vector.tensor_scalar(book[t][:, 0:V], book[t][:, 0:V], unit_sb[:, t : t + 1], 3.0, ALU.mult, ALU.mult)
 
         def fetch_ticks(t, r, on_vector):
             src = book[t][:].indirect(tick_sb[:, r * 16 : (r + 1) * 16])
@@ -303,9 +314,11 @@ def tile_picked_yofimb_tanh_p_kernel(
             finish(t)
             fetch_ticks(t, 0, False)
             fetch_ticks(t, 1, False)
-        for t in (2, 3):
-            weigh(t)
-            sum_flow(flow_bank_of[t], t)
+        weigh(2, whole)
+        sum_flow(flow_bank_of[2], 2)
+        for h in range(HALVES):
+            weigh(3, slice(h * HALF, (h + 1) * HALF))
+        sum_flow(flow_bank_of[3], 3)
         finish(2)
         finish(3)
         for r in range(2):
@@ -322,7 +335,7 @@ def tile_picked_yofimb_tanh_p_kernel(
                 hid_round[:].rearrange("p (r t) -> p r t", t=PACK), picked[:, :, cols].rearrange("p t r -> p r t")
             )
             nc.vector.quantize_mx(out=hid_codes[:].bitcast(FP8X4), scales=hid_bytes[:], in_=hid_round[:])
-            last = psum.tile([P, 256], F32, name="last", tag="bank%d01" % r)
+            last = psum.tile([P, 256], F32, name="last", tag="bank%d" % r)
             nc.tensor.matmul_mx(
                 out=last[:],
                 lhsT=w3_codes[:].bitcast(FP8X4),

@@ -75,15 +75,23 @@ def tile_picked_yofimb_tanh_p_kernel(
             nc.sync.dma_start(decay_sb[t][:], decay_dealt[t])
 
         x_codes = {}
+        listed_bytes = {}
         x_bytes = {}
 
         def gather_words(o, h):
             x_codes[o, h] = keep.tile([P, HALF], U32, name="x_codes%d%d" % (o, h), align_bytes=64)
-            nc.vector.tensor_copy(x_codes[o, h][:], x_table[o][:].indirect(offs_sb[:, h * 32 : (h + 1) * 32]))
+            dealt = x_codes[o, h][:].rearrange("p (d v) -> p v d", d=D)
+            nc.vector.tensor_copy(dealt, x_table[o][:].indirect(offs_sb[:, h * 32 : (h + 1) * 32]))
 
         def gather_bytes(h):
+            listed_bytes[h] = keep.tile([P, HALF], U8, name="listed_bytes%d" % h)
+            nc.vector.tensor_copy(listed_bytes[h][:], scale_table[:].indirect(offs_sb[:, h * 32 : (h + 1) * 32]))
+
+        def deal_bytes(h):
             x_bytes[h] = keep.tile([P, HALF], U8, name="x_bytes%d" % h, align_bytes=64)
-            nc.vector.tensor_copy(x_bytes[h][:], scale_table[:].indirect(offs_sb[:, h * 32 : (h + 1) * 32]))
+            nc.vector.tensor_copy(
+                x_bytes[h][:].rearrange("p (d v) -> p v d", d=D), listed_bytes[h][:].rearrange("p (v d) -> p v d", d=D)
+            )
 
         w_round = {}
         w_codes = {}
@@ -109,8 +117,10 @@ def tile_picked_yofimb_tanh_p_kernel(
         gather_words(0, 1)
         gather_bytes(0)
         gather_words(1, 0)
+        deal_bytes(0)
         gather_bytes(1)
         gather_words(1, 1)
+        deal_bytes(1)
         round_weight(0, 0, 0, False)
         quantise_weight(0, 0, 0)
         round_weight(0, 1, 0, False)
@@ -142,18 +152,17 @@ def tile_picked_yofimb_tanh_p_kernel(
         soft = [keep.tile([P, 4, HALF], F32, name="soft%d" % t) for t in range(PACK)]
         diff = [keep.tile([P, S], F32, name="diff%d" % t) for t in range(PACK)]
         flow = [keep.tile([P, S], F32, name="flow%d" % t) for t in range(PACK)]
+        weighted = [keep.tile([P, S], F32, name="weighted%d" % t) for t in range(PACK)]
         book = [keep.tile([P, 2 * V], F32, name="book%d" % t) for t in range(PACK)]
         inverse = keep.tile([P, PACK, V], F32, name="inverse")
         ident = keep.tile([P, P], F32, name="ident")
         make_identity(nc, ident[:])
-        parked = keep.tile([P, D, P], F32, name="parked")
+        parked = keep.tile([P, HALF], F32, name="parked")
         parked_unit = (0, 2, 0)
 
         def sigmoid(m, t, h):
             k = (t % 2) * 4 + h * 2 + m
-            src = banks[m, t, h][:].rearrange("p (v d) -> p d v", d=D)
-            dst = sig[:, k * HALF : (k + 1) * HALF].rearrange("p (d v) -> p d v", d=D)
-            nc.scalar.activation(dst, src, ACT.Sigmoid, scale=-1.0)
+            nc.scalar.activation(sig[:, k * HALF : (k + 1) * HALF], banks[m, t, h][:], ACT.Sigmoid, scale=-1.0)
 
         def logarithm(t, h):
             k = (t % 2) * 4 + h * 2
@@ -161,21 +170,15 @@ def tile_picked_yofimb_tanh_p_kernel(
             nc.scalar.activation(dst, sig[:, k * HALF : (k + 2) * HALF], ACT.Ln, bias=LN_FLOOR)
 
         def softplus(m, t, h):
-            part = soft[t][:, h * 2 + m, :].rearrange("p (d v) -> p d v", d=D)
-            if (m, t, h) == parked_unit:
-                raw = parked[:]
-            else:
-                raw = banks[m, t, h][:].rearrange("p (v d) -> p d v", d=D)
+            part = soft[t][:, h * 2 + m, :]
+            raw = parked[:] if (m, t, h) == parked_unit else banks[m, t, h][:]
             nc.vector.scalar_tensor_tensor(part, part, -1.0, raw, ALU.mult, ALU.max)
 
         def differ(t):
-            dealt = flow[t][:].rearrange("p (h c) -> p h c", h=HALVES)
-            sides = soft[t][:].rearrange("p (h m) c -> p m h c", m=2)
-            nc.vector.tensor_tensor(dealt, sides[:, 0], sides[:, 1], ALU.subtract)
-            nc.vector.tensor_copy(
-                diff[t][:].rearrange("p (h v d) -> p h v d", h=HALVES, d=D),
-                flow[t][:].rearrange("p (h d v) -> p h v d", h=HALVES, d=D),
-            )
+            for h in range(HALVES):
+                sides = [soft[t][:, h * 2 + m, :].rearrange("p (d c i) -> p c d i", d=D, i=4) for m in range(2)]
+                dst = diff[t][:, h * HALF : (h + 1) * HALF].rearrange("p (c i d) -> p c d i", d=D, i=4)
+                nc.vector.tensor_tensor(dst, sides[0], sides[1], ALU.subtract)
 
         def fetch_earlier(t, h, on_vector):
             src = diff[t][:].indirect(prv_sb[:, h * 32 : (h + 1) * 32])
@@ -187,7 +190,12 @@ def tile_picked_yofimb_tanh_p_kernel(
 
         def weigh(t, cols):
             nc.vector.tensor_tensor(flow[t][:, cols], diff[t][:, cols], flow[t][:, cols], ALU.subtract)
-            nc.vector.tensor_tensor(flow[t][:, cols], flow[t][:, cols], decay_sb[t][:, cols], ALU.mult)
+            nc.vector.tensor_tensor(
+                weighted[t][:, cols].rearrange("p (h d v) -> p h v d", d=D, v=P),
+                flow[t][:, cols].rearrange("p (h v d) -> p h v d", d=D, v=P),
+                decay_sb[t][:, cols].rearrange("p (h v d) -> p h v d", d=D, v=P),
+                ALU.mult,
+            )
 
         def add_turned(dst, blocks):
             for n, block in enumerate(blocks):
@@ -198,10 +206,9 @@ def tile_picked_yofimb_tanh_p_kernel(
                 blocks = [soft[t][:, h * 2 + m, d * P : (d + 1) * P] for m in range(2) for d in range(D)]
                 add_turned(bank[:, (t % 2) * 2 + h, :], blocks)
 
-        def sum_flow(bank, t):
-            for h in range(HALVES):
-                blocks = [flow[t][:, h * HALF + d : (h + 1) * HALF : D] for d in range(D)]
-                add_turned(bank[:, (t % 2) * 2 + h, :], blocks)
+        def sum_flow(t, h):
+            blocks = [weighted[t][:, (h * D + d) * P : (h * D + d + 1) * P] for d in range(D)]
+            add_turned(flow_bank_of[t, h][:, (t % 2) * 2 + h, :], blocks)
 
         first = [(0, 0), (0, 1), (1, 0), (1, 1)]
         for o in range(PASSES):
@@ -241,7 +248,7 @@ def tile_picked_yofimb_tanh_p_kernel(
                 for o in range(PASSES):
                     product(*second[n - 1], o, n)
         sigmoid(*second[0])
-        nc.vector.tensor_copy(parked[:], banks[parked_unit][:].rearrange("p (v d) -> p d v", d=D))
+        nc.vector.tensor_copy(parked[:], banks[parked_unit][:])
         for o in range(PASSES):
             product(*second[7], o, 1)
         for unit_mth in second[1:]:
@@ -279,28 +286,27 @@ def tile_picked_yofimb_tanh_p_kernel(
                 softplus(m, t, h)
             sum_depth(depth_second, t)
             differ(t)
-            fetch_earlier(t, 0, False)
+            fetch_earlier(t, 0, t == 3)
             fetch_earlier(t, 1, False)
         log_depth(1, depth_second)
         nc.scalar.activation(inverse[:], inverse[:], ACT.Exp, scale=-1.0)
-        flow_banks = [psum.tile([P, 4, P], F32, name="flow_bank", tag=tag) for tag in ("bank0", "bank2", "bank3")]
-        flow_bank_of = [flow_banks[0], flow_banks[0], flow_banks[1], flow_banks[2]]
-        sum_flow(flow_bank_of[0], 0)
-        sum_flow(flow_bank_of[1], 1)
+        flow_banks = [psum.tile([P, 4, P], F32, name="flow_bank", tag=tag) for tag in ("bank0", "bank2", "bank3", "bank4")]
+        flow_bank_of = {(t, h): flow_banks[max(0, t - 1) + (h if t == 3 else 0)] for t in range(PACK) for h in range(HALVES)}
+        for t, h in first:
+            sum_flow(t, h)
 
         picked = keep.tile([P, PACK, U], F32, name="picked")
-        back_tags = ["bank4", "bank5", "bank6", "bank7"]
-        def finish(t):
+        back_tags = {(0, 0): "bank5", (1, 0): "bank6", (2, 0): "bank7", (3, 0): "bank5", (3, 1): "bank6"}
+        def finish(t, halves):
+            cols = slice(halves[0] * P, (halves[-1] + 1) * P)
             ratio = book[t][:, V : 2 * V]
-            k = (t % 2) * 2
-            nc.vector.tensor_tensor(
-                ratio, flow_bank_of[t][:, k : k + 2, :].rearrange("p k i -> p (k i)"), inverse[:, t, :], ALU.mult
-            )
-            back = psum.tile([P, V], F32, name="back", tag=back_tags[t])
-            for h in range(HALVES):
+            sums = flow_bank_of[t, halves[0]][:].rearrange("p k i -> p (k i)")[:, (t % 2) * V : (t % 2 + 1) * V]
+            nc.vector.tensor_tensor(ratio[:, cols], sums[:, cols], inverse[:, t, cols], ALU.mult)
+            back = psum.tile([P, V], F32, name="back", tag=back_tags[t, halves[0]])
+            for h in halves:
                 nc.tensor.transpose(back[:, h * P : (h + 1) * P], ratio[:, h * P : (h + 1) * P], ident[:])
-            nc.scalar.activation(book[t][:, 0:V], back[:], ACT.Tanh)
-            nc.vector.tensor_scalar(book[t][:, 0:V], book[t][:, 0:V], unit_sb[:, t : t + 1], 3.0, ALU.mult, ALU.mult)
+            nc.scalar.activation(book[t][:, cols], back[:, cols], ACT.Tanh)
+            nc.vector.tensor_scalar(book[t][:, cols], book[t][:, cols], unit_sb[:, t : t + 1], 3.0, ALU.mult, ALU.mult)
 
         def fetch_ticks(t, r, on_vector):
             src = book[t][:].indirect(tick_sb[:, r * 16 : (r + 1) * 16])
@@ -311,29 +317,30 @@ def tile_picked_yofimb_tanh_p_kernel(
                 nc.scalar.activation(dst, src, ACT.Copy)
 
         for t in range(2):
-            finish(t)
+            finish(t, (0, 1))
             fetch_ticks(t, 0, False)
             fetch_ticks(t, 1, False)
         weigh(2, whole)
-        sum_flow(flow_bank_of[2], 2)
+        for h in range(HALVES):
+            sum_flow(2, h)
         for h in range(HALVES):
             weigh(3, slice(h * HALF, (h + 1) * HALF))
-        sum_flow(flow_bank_of[3], 3)
-        finish(2)
-        finish(3)
-        for r in range(2):
-            fetch_ticks(2, r, True)
+            sum_flow(3, h)
+        finish(2, (0, 1))
+        finish(3, (0,))
+        finish(3, (1,))
+        fetch_ticks(2, 0, True)
+        fetch_ticks(2, 1, False)
         fetch_ticks(3, 0, False)
-        fetch_ticks(3, 1, False)
+        fetch_ticks(3, 1, True)
 
         for r in range(2):
             cols = slice(r * 256, (r + 1) * 256)
             hid_round = keep.tile([P, 256 * PACK], BF16, name="hid_round%d" % r, align_bytes=64)
             hid_codes = keep.tile([P, 256], U32, name="hid_codes%d" % r, align_bytes=64)
             hid_bytes = keep.tile([P, 256], U8, name="hid_bytes%d" % r, align_bytes=64)
-            nc.vector.tensor_copy(
-                hid_round[:].rearrange("p (r t) -> p r t", t=PACK), picked[:, :, cols].rearrange("p t r -> p r t")
-            )
+            copy = nc.vector.tensor_copy if r == 0 else nc.scalar.copy
+            copy(hid_round[:].rearrange("p (r t) -> p r t", t=PACK), picked[:, :, cols].rearrange("p t r -> p r t"))
             nc.vector.quantize_mx(out=hid_codes[:].bitcast(FP8X4), scales=hid_bytes[:], in_=hid_round[:])
             last = psum.tile([P, 256], F32, name="last", tag="bank%d" % r)
             nc.tensor.matmul_mx(
@@ -346,5 +353,5 @@ def tile_picked_yofimb_tanh_p_kernel(
                 stop=True,
             )
             result = keep.tile([P, 256], F32, name="result%d" % r)
-            nc.scalar.copy(result[:], last[:])
+            copy(result[:], last[:])
             nc.sync.dma_start(out[:, cols], result[:])

@@ -98,7 +98,8 @@ def tile_picked_yofimb_tanh_p_kernel(
         w_bytes = {}
 
         def round_weight(m, o, g, on_vector):
-            w_round[m, o, g] = keep.tile([P, 2 * P * PACK], BF16, name="w_round%d%d%d" % (m, o, g), align_bytes=64)
+            tag = "vector_round" if on_vector else "scalar_round%d%d%d" % (m, o, g)
+            w_round[m, o, g] = keep.tile([P, 2 * P * PACK], BF16, name="w_round", tag=tag, align_bytes=64)
             dst = w_round[m, o, g][:].rearrange("p (t c j) -> p c t j", t=2, j=PACK)
             src = w_raw[m][o][:].rearrange("p j (c t) -> p c t j", t=PACK)[:, :, 2 * g : 2 * g + 2, :]
             if on_vector:
@@ -115,10 +116,10 @@ def tile_picked_yofimb_tanh_p_kernel(
 
         gather_words(0, 0)
         gather_words(0, 1)
-        gather_bytes(0)
         gather_words(1, 0)
-        deal_bytes(0)
+        gather_bytes(0)
         gather_bytes(1)
+        deal_bytes(0)
         gather_words(1, 1)
         deal_bytes(1)
         round_weight(0, 0, 0, False)
@@ -188,14 +189,17 @@ def tile_picked_yofimb_tanh_p_kernel(
             else:
                 nc.scalar.activation(dst, src, ACT.Copy)
 
-        def weigh(t, cols):
-            nc.vector.tensor_tensor(flow[t][:, cols], diff[t][:, cols], flow[t][:, cols], ALU.subtract)
-            nc.vector.tensor_tensor(
-                weighted[t][:, cols].rearrange("p (h d v) -> p h v d", d=D, v=P),
-                flow[t][:, cols].rearrange("p (h v d) -> p h v d", d=D, v=P),
-                decay_sb[t][:, cols].rearrange("p (h v d) -> p h v d", d=D, v=P),
-                ALU.mult,
-            )
+        def weigh(t):
+            parts = [slice(h * HALF, (h + 1) * HALF) for h in range(HALVES)]
+            for cols in parts:
+                nc.vector.tensor_tensor(flow[t][:, cols], diff[t][:, cols], flow[t][:, cols], ALU.subtract)
+            for cols in parts:
+                nc.vector.tensor_tensor(
+                    weighted[t][:, cols].rearrange("p (d v) -> p v d", d=D),
+                    flow[t][:, cols].rearrange("p (v d) -> p v d", d=D),
+                    decay_sb[t][:, cols].rearrange("p (v d) -> p v d", d=D),
+                    ALU.mult,
+                )
 
         def add_turned(dst, blocks):
             for n, block in enumerate(blocks):
@@ -223,19 +227,16 @@ def tile_picked_yofimb_tanh_p_kernel(
         for t, h in ask_order:
             sigmoid(1, t, h)
 
-        round_weight(0, 1, 1, True)
         quantise_weight(0, 0, 1)
-        round_weight(1, 0, 1, True)
-        quantise_weight(0, 1, 1)
-        round_weight(1, 1, 1, True)
-        quantise_weight(1, 0, 1)
+        for m, o in ((0, 1), (1, 0), (1, 1)):
+            round_weight(m, o, 1, True)
+            quantise_weight(m, o, 1)
         w3_round = keep.tile([P, N * PACK], BF16, name="w3_round", align_bytes=64)
         w3_codes = keep.tile([P, N], U32, name="w3_codes", align_bytes=64)
         w3_bytes = keep.tile([P, N], U8, name="w3_bytes", align_bytes=64)
         nc.vector.tensor_copy(
             w3_round[:].rearrange("p (n j) -> p n j", j=PACK), w3_raw[:].rearrange("p j n -> p n j")
         )
-        quantise_weight(1, 1, 1)
         nc.vector.quantize_mx(out=w3_codes[:].bitcast(FP8X4), scales=w3_bytes[:], in_=w3_round[:])
 
         units = [(m, h) for h in range(HALVES) for m in range(2)]
@@ -265,15 +266,14 @@ def tile_picked_yofimb_tanh_p_kernel(
         depth_first = psum.tile([P, 4, P], F32, name="depth_first", tag="bank0")
         sum_depth(depth_first, 0)
         sum_depth(depth_first, 1)
-        whole = slice(0, S)
         differ(0)
         differ(1)
         fetch_earlier(0, 0, True)
         fetch_earlier(0, 1, True)
         fetch_earlier(1, 0, False)
         fetch_earlier(1, 1, False)
-        weigh(0, whole)
-        weigh(1, whole)
+        weigh(0)
+        weigh(1)
 
         logarithm(2, 1)
         logarithm(2, 0)
@@ -320,12 +320,10 @@ def tile_picked_yofimb_tanh_p_kernel(
             finish(t, (0, 1))
             fetch_ticks(t, 0, False)
             fetch_ticks(t, 1, False)
-        weigh(2, whole)
-        for h in range(HALVES):
-            sum_flow(2, h)
-        for h in range(HALVES):
-            weigh(3, slice(h * HALF, (h + 1) * HALF))
-            sum_flow(3, h)
+        for t in (2, 3):
+            weigh(t)
+            for h in range(HALVES):
+                sum_flow(t, h)
         finish(2, (0, 1))
         finish(3, (0,))
         finish(3, (1,))

from contextlib import ExitStack

import concourse.mybir as mybir
from concourse.masks import make_identity

K, T, S, D, N, H, V, U = 1024, 2048, 1024, 4, 128, 512, 256, 512
FLOPS = 2 * (2 * K * H * S + H * N * U)

F32 = mybir.dt.float32
BF16 = mybir.dt.bfloat16
I32 = mybir.dt.int32
U32 = mybir.dt.uint32
U16 = mybir.dt.uint16
U8 = mybir.dt.uint8
FP8X4 = mybir.dt.float8_e4m3fn_x4
ALU = mybir.AluOpType
ACT = mybir.ActivationFunctionType

P = 128
PACK = 4
PASSES = K // (P * PACK)
HALF = 512
HALVES = S // HALF
LN_FLOOR = 2.0 ** -60


def tile_picked_yofimb_tanh_p_kernel(
    tc, x_words, x_scales, w1, w2, decay, unit, w3, offs, prv, tick, out
):
    nc = tc.nc
    with ExitStack() as ctx:
        keep = ctx.enter_context(tc.tile_pool(name="keep", bufs=1))
        psum = ctx.enter_context(tc.psum_pool(name="psum", bufs=1))

        offs_sb = keep.tile([P, S // 16], U16, name="offs_sb")
        prv_sb = keep.tile([P, S // 16], U16, name="prv_sb")
        tick_sb = keep.tile([P, U // 16], U16, name="tick_sb")
        x_table = [keep.tile([P, T], U32, name="x_table%d" % o) for o in range(PASSES)]
        scale_table = keep.tile([P, T], U8, name="scale_table")
        weights = (w1, w2)
        w_raw = [[keep.tile([P, PACK, H], F32, name="w_raw%d%d" % (m, o)) for o in range(PASSES)] for m in range(2)]
        decay_sb = [keep.tile([P, S], F32, name="decay%d" % t) for t in range(PACK)]
        unit_sb = keep.tile([P, PACK], F32, name="unit_sb")
        w3_raw = keep.tile([P, PACK, N], F32, name="w3_raw")

        def load_words(o):
            nc.sync.dma_start(x_table[o][:].bitcast(I32), x_words[o].rearrange("p c r -> p (c r)").bitcast(I32))

        def load_weight(m, o):
            rows = weights[m][o * P * PACK : (o + 1) * P * PACK, :]
            nc.sync.dma_start(w_raw[m][o][:], rows.rearrange("(p j) c -> p j c", j=PACK))

        nc.vector.memset(scale_table[:].bitcast(I32), 0)
        warm = keep.tile([P, 2], F32, name="warm")
        nc.vector.memset(warm[:, 0:1], 0.0)
        nc.scalar.activation(warm[:, 1:2], warm[:, 0:1], ACT.Sigmoid, scale=-1.0)
        nc.sync.dma_start(offs_sb[:], offs)
        load_words(0)
        for q in range(4):
            nc.sync.dma_start(
                scale_table[32 * q : 32 * q + 4 * PASSES, :].bitcast(I32),
                x_scales[:, 4 * q : 4 * q + 4, :].bitcast(I32),
            )
        load_words(1)
        load_weight(0, 0)
        load_weight(0, 1)
        load_weight(1, 0)
        load_weight(1, 1)
        nc.sync.dma_start(prv_sb[:], prv)
        nc.sync.dma_start(tick_sb[:], tick)
        nc.sync.dma_start(unit_sb[:], unit.rearrange("(p t) o -> p (t o)", t=PACK))
        nc.sync.dma_start(w3_raw[:], w3.rearrange("(p j) n -> p j n", j=PACK))
        decay_dealt = decay.rearrange("(p t) j -> t p j", t=PACK)
        for t in range(PACK):
            nc.sync.dma_start(decay_sb[t][:], decay_dealt[t])

        x_codes = {}
        listed_bytes = {}
        x_bytes = {}

        def gather_words(o, h):
            x_codes[o, h] = keep.tile([P, HALF], U32, name="x_codes%d%d" % (o, h), align_bytes=64)
            dealt = x_codes[o, h][:].rearrange("p (d v) -> p v d", d=D)
            nc.vector.tensor_copy(dealt, x_table[o][:].indirect(offs_sb[:, h * 32 : (h + 1) * 32]))

        def gather_bytes(h):
            listed_bytes[h] = keep.tile([P, HALF], U8, name="listed_bytes%d" % h)
            nc.vector.tensor_copy(listed_bytes[h][:], scale_table[:].indirect(offs_sb[:, h * 32 : (h + 1) * 32]))

        def deal_bytes(h):
            x_bytes[h] = keep.tile([P, HALF], U8, name="x_bytes%d" % h, align_bytes=64)
            nc.vector.tensor_copy(
                x_bytes[h][:].rearrange("p (d v) -> p v d", d=D), listed_bytes[h][:].rearrange("p (v d) -> p v d", d=D)
            )

        w_round = {}
        w_codes = {}
        w_bytes = {}

        def round_weight(m, o, g, on_vector):
            tag = "vector_round" if on_vector else "scalar_round%d%d%d" % (m, o, g)
            w_round[m, o, g] = keep.tile([P, 2 * P * PACK], BF16, name="w_round", tag=tag, align_bytes=64)
            dst = w_round[m, o, g][:].rearrange("p (t c j) -> p c t j", t=2, j=PACK)
            src = w_raw[m][o][:].rearrange("p j (c t) -> p c t j", t=PACK)[:, :, 2 * g : 2 * g + 2, :]
            if on_vector:
                nc.vector.tensor_copy(dst, src)
            else:
                nc.scalar.copy(dst, src)

        def quantise_weight(m, o, g):
            w_codes[m, o, g] = keep.tile([P, 2 * P], U32, name="w_codes%d%d%d" % (m, o, g), align_bytes=64)
            w_bytes[m, o, g] = keep.tile([P, 2 * P], U8, name="w_bytes%d%d%d" % (m, o, g), align_bytes=64)
            nc.vector.quantize_mx(
                out=w_codes[m, o, g][:].bitcast(FP8X4), scales=w_bytes[m, o, g][:], in_=w_round[m, o, g][:]
            )

        gather_words(0, 0)
        gather_words(0, 1)
        gather_words(1, 0)
        gather_bytes(0)
        gather_bytes(1)
        deal_bytes(0)
        gather_words(1, 1)
        deal_bytes(1)
        round_weight(0, 0, 0, False)
        quantise_weight(0, 0, 0)
        round_weight(0, 1, 0, False)
        quantise_weight(0, 1, 0)
        round_weight(1, 0, 0, False)
        quantise_weight(1, 0, 0)
        round_weight(1, 1, 0, True)
        quantise_weight(1, 1, 0)
        round_weight(0, 0, 1, False)

        banks = {}

        def product(m, t, h, o, bank):
            g, tl = divmod(t, 2)
            if o == 0:
                banks[m, t, h] = psum.tile([P, HALF], F32, name="bank", tag="bank%d" % bank)
            cols = slice(tl * P, (tl + 1) * P)
            nc.tensor.matmul_mx(
                out=banks[m, t, h][:],
                lhsT=w_codes[m, o, g][:, cols].bitcast(FP8X4),
                lhsT_scale=w_bytes[m, o, g][:, cols],
                rhs=x_codes[o, h][:].bitcast(FP8X4),
                rhs_scale=x_bytes[h][4 * o : P, :],
                start=(o == 0),
                stop=(o == PASSES - 1),
            )

        sig = keep.tile([P, 8 * HALF], F32, name="sig")
        soft = [keep.tile([P, 4, HALF], F32, name="soft%d" % t) for t in range(PACK)]
        diff = [keep.tile([P, S], F32, name="diff%d" % t) for t in range(PACK)]
        flow = [keep.tile([P, S], F32, name="flow%d" % t) for t in range(PACK)]
        weighted = [keep.tile([P, S], F32, name="weighted%d" % t) for t in range(PACK)]
        book = [keep.tile([P, 2 * V], F32, name="book%d" % t) for t in range(PACK)]
        inverse = keep.tile([P, PACK, V], F32, name="inverse")
        ident = keep.tile([P, P], F32, name="ident")
        make_identity(nc, ident[:])
        parked = keep.tile([P, HALF], F32, name="parked")
        parked_unit = (0, 2, 0)

        def sigmoid(m, t, h):
            k = (t % 2) * 4 + h * 2 + m
            nc.scalar.activation(sig[:, k * HALF : (k + 1) * HALF], banks[m, t, h][:], ACT.Sigmoid, scale=-1.0)

        def logarithm(t, h):
            k = (t % 2) * 4 + h * 2
            dst = soft[t][:, h * 2 : h * 2 + 2, :].rearrange("p m c -> p (m c)")
            nc.scalar.activation(dst, sig[:, k * HALF : (k + 2) * HALF], ACT.Ln, bias=LN_FLOOR)

        def softplus(m, t, h):
            part = soft[t][:, h * 2 + m, :]
            raw = parked[:] if (m, t, h) == parked_unit else banks[m, t, h][:]
            nc.vector.scalar_tensor_tensor(part, part, -1.0, raw, ALU.mult, ALU.max)

        def differ(t):
            for h in range(HALVES):
                sides = [soft[t][:, h * 2 + m, :].rearrange("p (d c i) -> p c d i", d=D, i=4) for m in range(2)]
                dst = diff[t][:, h * HALF : (h + 1) * HALF].rearrange("p (c i d) -> p c d i", d=D, i=4)
                nc.vector.tensor_tensor(dst, sides[0], sides[1], ALU.subtract)

        def fetch_earlier(t, h, on_vector):
            src = diff[t][:].indirect(prv_sb[:, h * 32 : (h + 1) * 32])
            dst = flow[t][:, h * HALF : (h + 1) * HALF]
            if on_vector:
                nc.vector.tensor_copy(dst, src)
            else:
                nc.scalar.activation(dst, src, ACT.Copy)

        def weigh(t):
            parts = [slice(h * HALF, (h + 1) * HALF) for h in range(HALVES)]
            for cols in parts:
                nc.vector.tensor_tensor(flow[t][:, cols], diff[t][:, cols], flow[t][:, cols], ALU.subtract)
            for cols in parts:
                nc.vector.tensor_tensor(
                    weighted[t][:, cols].rearrange("p (d v) -> p v d", d=D),
                    flow[t][:, cols].rearrange("p (v d) -> p v d", d=D),
                    decay_sb[t][:, cols].rearrange("p (v d) -> p v d", d=D),
                    ALU.mult,
                )

        def add_turned(dst, blocks):
            for n, block in enumerate(blocks):
                nc.tensor.matmul(dst, block, ident[:], start=(n == 0), stop=(n == len(blocks) - 1), is_transpose=True)

        def sum_depth(bank, t):
            for h in range(HALVES):
                blocks = [soft[t][:, h * 2 + m, d * P : (d + 1) * P] for m in range(2) for d in range(D)]
                add_turned(bank[:, (t % 2) * 2 + h, :], blocks)

        def sum_flow(t, h):
            blocks = [weighted[t][:, (h * D + d) * P : (h * D + d + 1) * P] for d in range(D)]
            add_turned(flow_bank_of[t, h][:, (t % 2) * 2 + h, :], blocks)

        first = [(0, 0), (0, 1), (1, 0), (1, 1)]
        for o in range(PASSES):
            for t, h in first:
                product(0, t, h, o, t * 4 + h * 2)
        for t, h in first:
            sigmoid(0, t, h)
        ask_order = first[::-1]
        for o in range(PASSES):
            for t, h in ask_order:
                product(1, t, h, o, t * 4 + h * 2 + 1)
        for t, h in ask_order:
            sigmoid(1, t, h)

        quantise_weight(0, 0, 1)
        for m, o in ((0, 1), (1, 0), (1, 1)):
            round_weight(m, o, 1, True)
            quantise_weight(m, o, 1)
        w3_round = keep.tile([P, N * PACK], BF16, name="w3_round", align_bytes=64)
        w3_codes = keep.tile([P, N], U32, name="w3_codes", align_bytes=64)
        w3_bytes = keep.tile([P, N], U8, name="w3_bytes", align_bytes=64)
        nc.vector.tensor_copy(
            w3_round[:].rearrange("p (n j) -> p n j", j=PACK), w3_raw[:].rearrange("p j n -> p n j")
        )
        nc.vector.quantize_mx(out=w3_codes[:].bitcast(FP8X4), scales=w3_bytes[:], in_=w3_round[:])

        units = [(m, h) for h in range(HALVES) for m in range(2)]
        for t, h in first:
            logarithm(t, h)
        second = [(m, 2, h) for m, h in units[:3]] + [(m, 3, h) for m, h in units] + [(units[3][0], 2, units[3][1])]
        for n, (t, (m, h)) in enumerate((t, unit_mh) for t in range(2) for unit_mh in units):
            softplus(m, t, h)
            if n > 0:
                for o in range(PASSES):
                    product(*second[n - 1], o, n)
        sigmoid(*second[0])
        nc.vector.tensor_copy(parked[:], banks[parked_unit][:])
        for o in range(PASSES):
            product(*second[7], o, 1)
        for unit_mth in second[1:]:
            sigmoid(*unit_mth)

        def log_depth(g, bank):
            nc.scalar.activation(
                inverse[:, 2 * g : 2 * g + 2, :].rearrange("p t v -> p (t v)"),
                bank[:].rearrange("p k i -> p (k i)"),
                ACT.Ln,
                bias=1.0,
            )

        depth_first = psum.tile([P, 4, P], F32, name="depth_first", tag="bank0")
        sum_depth(depth_first, 0)
        sum_depth(depth_first, 1)
        differ(0)
        differ(1)
        fetch_earlier(0, 0, True)
        fetch_earlier(0, 1, True)
        fetch_earlier(1, 0, False)
        fetch_earlier(1, 1, False)
        weigh(0)
        weigh(1)

        logarithm(2, 1)
        logarithm(2, 0)
        log_depth(0, depth_first)
        logarithm(3, 0)
        logarithm(3, 1)
        depth_second = psum.tile([P, 4, P], F32, name="depth_second", tag="bank1")
        for t in (2, 3):
            for m, h in units[::-1] if t == 2 else units:
                softplus(m, t, h)
            sum_depth(depth_second, t)
            differ(t)
            fetch_earlier(t, 0, t == 3)
            fetch_earlier(t, 1, False)
        log_depth(1, depth_second)
        nc.scalar.activation(inverse[:], inverse[:], ACT.Exp, scale=-1.0)
        flow_banks = [psum.tile([P, 4, P], F32, name="flow_bank", tag=tag) for tag in ("bank0", "bank2", "bank3", "bank4")]
        flow_bank_of = {(t, h): flow_banks[max(0, t - 1) + (h if t == 3 else 0)] for t in range(PACK) for h in range(HALVES)}
        for t, h in first:
            sum_flow(t, h)

        picked = keep.tile([P, PACK, U], F32, name="picked")
        back_tags = {(0, 0): "bank5", (1, 0): "bank6", (2, 0): "bank7", (3, 0): "bank5", (3, 1): "bank6"}
        def finish(t, halves):
            cols = slice(halves[0] * P, (halves[-1] + 1) * P)
            ratio = book[t][:, V : 2 * V]
            sums = flow_bank_of[t, halves[0]][:].rearrange("p k i -> p (k i)")[:, (t % 2) * V : (t % 2 + 1) * V]
            nc.vector.tensor_tensor(ratio[:, cols], sums[:, cols], inverse[:, t, cols], ALU.mult)
            back = psum.tile([P, V], F32, name="back", tag=back_tags[t, halves[0]])
            for h in halves:
                nc.tensor.transpose(back[:, h * P : (h + 1) * P], ratio[:, h * P : (h + 1) * P], ident[:])
            nc.scalar.activation(book[t][:, cols], back[:, cols], ACT.Tanh)
            nc.vector.tensor_scalar(book[t][:, cols], book[t][:, cols], unit_sb[:, t : t + 1], 3.0, ALU.mult, ALU.mult)

        def fetch_ticks(t, r, on_vector):
            src = book[t][:].indirect(tick_sb[:, r * 16 : (r + 1) * 16])
            dst = picked[:, t, r * 256 : (r + 1) * 256]
            if on_vector:
                nc.vector.tensor_copy(dst, src)
            else:
                nc.scalar.activation(dst, src, ACT.Copy)

        for t in range(2):
            finish(t, (0, 1))
            fetch_ticks(t, 0, False)
            fetch_ticks(t, 1, False)
        for t in (2, 3):
            weigh(t)
            for h in range(HALVES):
                sum_flow(t, h)
        finish(2, (0, 1))
        finish(3, (0,))
        finish(3, (1,))
        fetch_ticks(2, 0, True)
        fetch_ticks(2, 1, False)
        fetch_ticks(3, 0, False)
        fetch_ticks(3, 1, True)

        for r in range(2):
            cols = slice(r * 256, (r + 1) * 256)
            hid_round = keep.tile([P, 256 * PACK], BF16, name="hid_round%d" % r, align_bytes=64)
            hid_codes = keep.tile([P, 256], U32, name="hid_codes%d" % r, align_bytes=64)
            hid_bytes = keep.tile([P, 256], U8, name="hid_bytes%d" % r, align_bytes=64)
            copy = nc.vector.tensor_copy if r == 0 else nc.scalar.copy
            copy(hid_round[:].rearrange("p (r t) -> p r t", t=PACK), picked[:, :, cols].rearrange("p t r -> p r t"))
            nc.vector.quantize_mx(out=hid_codes[:].bitcast(FP8X4), scales=hid_bytes[:], in_=hid_round[:])
            last = psum.tile([P, 256], F32, name="last", tag="bank%d" % r)
            nc.tensor.matmul_mx(
                out=last[:],
                lhsT=w3_codes[:].bitcast(FP8X4),
                lhsT_scale=w3_bytes[:],
                rhs=hid_codes[:].bitcast(FP8X4),
                rhs_scale=hid_bytes[:],
                start=True,
                stop=True,
            )
            result = keep.tile([P, 256], F32, name="result%d" % r)
            copy(result[:], last[:])
            nc.sync.dma_start(out[:, cols], result[:])
